import numpy as np
import ml_dtypes


def mxq(x, axis, fmt="e4m3"):
    dtype, down = {"e4m3": (ml_dtypes.float8_e4m3fn, 7), "e5m2": (ml_dtypes.float8_e5m2, 14)}[fmt]
    v = np.moveaxis(np.asarray(x, np.float32).astype(ml_dtypes.bfloat16).astype(np.float64), axis, -1)
    blocks = v.reshape(v.shape[:-1] + (-1, 32))
    amax = np.abs(blocks).max(-1, keepdims=True)
    byte = np.maximum(np.where(amax > 0, np.frexp(amax)[1] - 1 + 127, 0) - down, 1)
    scale = np.exp2(byte - 127.0)
    codes = (blocks / scale).astype(np.float32).astype(dtype).astype(np.float64)
    return np.moveaxis((codes * scale).reshape(v.shape), -1, axis)


WIDE = False


def mx_kscale(k):
    if not WIDE:
        return np.ones(k)
    levels = np.array([10, -10, 5, -5, 0])
    if k % 512:
        return np.exp2(np.random.permutation(np.resize(levels, k // 32))).repeat(32)
    a = np.empty((k // 512, 16))
    for p in range(k // 512):
        a[p, :8] = np.random.permutation(np.resize(levels, 8))
        for g in range(8):
            far = levels[np.abs(levels - a[p, g]) >= 10]
            a[p, g + 8] = far[np.random.randint(len(far))]
    return np.exp2(a.ravel()).repeat(32)


def f64(x):
    return np.asarray(x).astype(np.float64)


def striped(idx):
    return np.tile(idx.reshape(-1, 16).T, (8, 1)).astype(np.uint16)


def unstriped(offs):
    return offs[:16].T.reshape(-1).astype(np.int64)


def striped8(idx):
    return np.concatenate([x.reshape(-1, 16).T for x in idx]).astype(np.uint16)


def runs(offs, k):
    lists = np.stack([offs[16 * r : 16 * r + 16].T.reshape(-1) for r in range(8)]).astype(np.int64)
    return lists[np.arange(k) % 512 // 64]


def pack_weight(w):
    k, n = w.shape
    w = f64(np.asarray(w, np.float32).astype(ml_dtypes.bfloat16)).reshape(k // 32, 32, n)
    amax = np.abs(w).max(1)
    byte = np.clip(np.where(amax > 0, np.frexp(amax)[1] - 1 + 127 - 7, 1), 1, 254)
    scaled = (w * np.exp2(127.0 - byte)[:, None, :]).reshape(k, n).astype(np.float32)
    words = np.ascontiguousarray(scaled.reshape(k // 512, 128, 4, n).transpose(0, 1, 3, 2)).astype(ml_dtypes.float8_e4m3fn).view(np.uint8)
    return words, np.ascontiguousarray(byte.astype(np.uint8).reshape(k // 512, 16, n))


def unpack_weight(words, scales):
    g, p, n, _ = words.shape
    vals = np.ascontiguousarray(words).view(ml_dtypes.float8_e4m3fn).astype(np.float64) * np.repeat(np.exp2(scales.astype(np.float64) - 127.0), 8, axis=1)[..., None]
    return vals.transpose(0, 1, 3, 2).reshape(g * 512, n)


def sigmoid(v):
    return 1.0 / (1.0 + np.exp(-np.maximum(v, -700.0)))


K, T, S, N, H = 512, 2048, 512, 512, 512


def setup_inputs():
    n = np.random.standard_normal
    s = mx_kscale(K)[:, None]
    u = mx_kscale(S)
    packed_xT = pack_weight(n((K, T)) * s)
    return {
        "x_words": packed_xT[0],
        "x_scales": packed_xT[1],
        "wa": (n((K, H)) / np.sqrt(K) / s).astype(np.float32),
        "wb": (n((K, N)) / np.sqrt(K) / s).astype(np.float32),
        "gt": (np.random.uniform(0.5, 1.5, (S, 1)) * u[:, None]).astype(np.float32),
        "gi": (np.random.uniform(0.5, 1.5, (S, 1)) / u[:, None]).astype(np.float32),
        "offs": striped(np.random.permutation(T)[:S]),
        "two": striped(np.random.permutation(T)[:S]),
        "n1": striped8(np.stack([np.random.permutation(H) for _ in range(8)])),
        "n2": striped8(np.stack([np.random.permutation(H) for _ in range(8)])),
        "n3": striped8(np.stack([np.random.permutation(N) for _ in range(8)])),
    }


def reference(x_words, x_scales, wa, wb, gt, gi, offs, two, n1, n2, n3):
    xq = unpack_weight(x_words, x_scales)[:, unstriped(offs)]
    a = xq.T @ mxq(f64(wa), 0, "e4m3")
    z = f64(gt) * (np.maximum(a * (sigmoid(a[np.arange(S)[:, None], runs(n1, S)])), a[np.arange(S)[:, None], runs(n2, S)]))
    x_two = unpack_weight(x_words, x_scales)[:, unstriped(two)]
    b = x_two.T @ mxq(f64(wb), 0, "e4m3")
    z2 = f64(gi) * b
    cv = 0.0625 * ((mxq(z, 0, "e4m3").T @ mxq(z2, 0, "e4m3")))
    st = cv - (cv[np.arange(H)[:, None], runs(n3, H)])
    return st - (0.5 * (st[np.arange(H)[:, None], runs(n3, H)]))

@@ -1,0 +1,169 @@
+from contextlib import ExitStack
+
+import concourse.mybir as mybir
+
+K, T, S, N, H = 512, 2048, 512, 512, 512
+FLOPS = 2 * K * S * H + 2 * K * S * N + 2 * S * H * N
+
+F32 = mybir.dt.float32
+BF16 = mybir.dt.bfloat16
+I32 = mybir.dt.int32
+U32 = mybir.dt.uint32
+U16 = mybir.dt.uint16
+U8 = mybir.dt.uint8
+FP8X4 = mybir.dt.float8_e4m3fn_x4
+ALU = mybir.AluOpType
+ACT = mybir.ActivationFunctionType
+
+P = 128
+PACK = 4
+WIN = 1024
+
+
+def tile_picked_momgmaxtwice_none_p_kernel(tc, x_words, x_scales, wa, wb, gt, gi, offs, two, n1, n2, n3, out):
+    nc = tc.nc
+    with ExitStack() as ctx:
+        keep = ctx.enter_context(tc.tile_pool(name="keep", bufs=1))
+        psum = ctx.enter_context(tc.psum_pool(name="psum", bufs=1))
+
+        def tl(shape, dt, name):
+            return keep.tile(shape, dt, name=name, align_bytes=64)
+
+        lists = {}
+        for name in ("offs", "two", "n1", "n2", "n3"):
+            lists[name] = keep.tile([P, S // 16], U16, name="list_" + name)
+        xs = tl([P, T], U8, "xs")
+        xw = tl([P, T], U32, "xw")
+        nc.vector.memset(xs[:].bitcast(I32), 0)
+
+        half = H // 2
+        wa_raw = [tl([P, PACK, half], F32, "wa_raw%d" % h) for h in range(2)]
+        wb_raw = [tl([P, PACK, half], F32, "wb_raw%d" % h) for h in range(2)]
+        gt_sb = tl([P, PACK], F32, "gt_sb")
+        gi_sb = tl([P, PACK], F32, "gi_sb")
+
+        nc.sync.dma_start(lists["offs"][:], offs)
+        for q in range(4):
+            nc.scalar.dma_start(xs[32 * q : 32 * q + 4, :].bitcast(I32), x_scales[0, 4 * q : 4 * q + 4, :].bitcast(I32))
+        nc.sync.dma_start(xw[:].bitcast(I32), x_words[0].rearrange("p n t -> p (n t)").bitcast(I32))
+        nc.sync.dma_start(lists["two"][:], two)
+        wa_v = wa.rearrange("(p j) c -> p j c", j=PACK)
+        wb_v = wb.rearrange("(p j) c -> p j c", j=PACK)
+        for h in range(2):
+            nc.sync.dma_start(wa_raw[h][:], wa_v[:, :, h * half : (h + 1) * half])
+        nc.sync.dma_start(gt_sb[:], gt.rearrange("(p t) o -> p (t o)", t=PACK))
+        nc.sync.dma_start(gi_sb[:], gi.rearrange("(p t) o -> p (t o)", t=PACK))
+        nc.sync.dma_start(lists["n1"][:], n1)
+        nc.sync.dma_start(lists["n2"][:], n2)
+        for h in range(2):
+            nc.sync.dma_start(wb_raw[h][:], wb_v[:, :, h * half : (h + 1) * half])
+        nc.sync.dma_start(lists["n3"][:], n3)
+
+        win_a = [tl([P, WIN], F32, "win_a%d" % t) for t in range(PACK)]
+        win_c = [tl([P, WIN], F32, "win_c%d" % t) for t in range(PACK)]
+        for t in range(PACK):
+            nc.vector.memset(win_a[t][:, H:WIN], 0.0)
+            nc.vector.memset(win_c[t][:, H:WIN], 0.0)
+
+        warm = tl([P, 1], F32, "warm")
+        nc.scalar.activation(warm[:], win_a[0][:, H : H + 1], ACT.Sigmoid)
+
+        sgn2 = tl([P, PACK], F32, "sgn2")
+        sgn = tl([P, PACK], F32, "sgn")
+        gt_abs = tl([P, PACK], F32, "gt_abs")
+        gi_sgn = tl([P, PACK], F32, "gi_sgn")
+        nc.gpsimd.tensor_scalar(sgn2[:], gt_sb[:], 0.0, 2.0, ALU.is_ge, ALU.mult)
+        nc.gpsimd.tensor_scalar(sgn[:], sgn2[:], 1.0, -1.0, ALU.mult, ALU.add)
+        nc.gpsimd.tensor_tensor(gt_abs[:], gt_sb[:], sgn[:], ALU.mult)
+        nc.gpsimd.tensor_tensor(gi_sgn[:], gi_sb[:], sgn[:], ALU.mult)
+
+        words = {}
+        scales = {}
+        for name in ("offs", "two"):
+            picked = tl([P, S], U8, "picked_" + name)
+            scales[name] = tl([P, S], U8, "scales_" + name)
+            nc.vector.tensor_copy(picked[:], xs[:].indirect(lists[name][:]))
+            nc.vector.tensor_copy(scales[name][:].rearrange("p (t m) -> p t m", t=PACK), picked[:].rearrange("p (m t) -> p t m", t=PACK))
+        for name in ("offs", "two"):
+            words[name] = tl([P, S], U32, "words_" + name)
+            nc.vector.tensor_copy(words[name][:].rearrange("p (t m) -> p m t", t=PACK), xw[:].indirect(lists[name][:]))
+
+        def interleave(copy, dst, raw, h):
+            copy(
+                dst[:, h * half * PACK : (h + 1) * half * PACK].rearrange("p (c i t) -> p c t i", i=4, t=PACK),
+                raw[:].rearrange("p t (c i) -> p c t i", i=4),
+            )
+
+        wa_bf = tl([P, H * PACK], BF16, "wa_bf")
+        wa_q = tl([P, H], U32, "wa_q")
+        wa_s = tl([P, H], U8, "wa_s")
+        for h in range(2):
+            interleave(nc.scalar.copy, wa_bf, wa_raw[h], h)
+        nc.vector.quantize_mx(out=wa_q[:].bitcast(FP8X4), scales=wa_s[:], in_=wa_bf[:])
+
+        banks = [psum.tile([P, 512], F32, name="bank%d" % b) for b in range(8)]
+        for t in range(PACK):
+            cols = slice(t * P, (t + 1) * P)
+            nc.tensor.matmul_mx(out=banks[t][:], lhsT=words["offs"][:, cols].bitcast(FP8X4), lhsT_scale=scales["offs"][:, cols],
+                                rhs=wa_q[:].bitcast(FP8X4), rhs_scale=wa_s[:], start=True, stop=True)
+
+        wb_bf = tl([P, N * PACK], BF16, "wb_bf")
+        wb_q = tl([P, N], U32, "wb_q")
+        wb_s = tl([P, N], U8, "wb_s")
+        interleave(nc.scalar.copy, wb_bf, wb_raw[0], 0)
+        interleave(nc.vector.tensor_copy, wb_bf, wb_raw[1], 1)
+        nc.vector.quantize_mx(out=wb_q[:].bitcast(FP8X4), scales=wb_s[:], in_=wb_bf[:])
+        for c in range(4):
+            ncols = slice(c * P, (c + 1) * P)
+            for t in range(PACK):
+                cols = slice(t * P, (t + 1) * P)
+                nc.tensor.matmul_mx(out=banks[4 + c][:, cols], lhsT=words["two"][:, cols].bitcast(FP8X4), lhsT_scale=scales["two"][:, cols],
+                                    rhs=wb_q[:, ncols].bitcast(FP8X4), rhs_scale=wb_s[:, ncols], start=True, stop=True)
+
+        sig = [tl([P, H], F32, "sig%d" % t) for t in range(PACK)]
+        prod = tl([P, PACK, H], F32, "prod")
+        other = tl([P, PACK, H], F32, "other")
+        z2_bf = tl([P, N * PACK], BF16, "z2_bf")
+        gi_b = gi_sgn[:].rearrange("p (a t) -> p a t", a=1).to_broadcast([P, P, PACK])
+        for t in range(PACK):
+            nc.scalar.activation(win_c[t][:, 0:H], banks[t][:], ACT.Copy, scale=gt_abs[:, t : t + 1])
+            nc.scalar.copy(win_a[t][:, 0:H], banks[t][:])
+            nc.scalar.activation(sig[t][:], win_a[t][:].indirect(lists["n1"][:]), ACT.Sigmoid)
+            nc.vector.tensor_copy(other[:, t, :], win_c[t][:].indirect(lists["n2"][:]))
+            nc.vector.tensor_tensor(
+                z2_bf[:, t * P * PACK : (t + 1) * P * PACK].rearrange("p (n t) -> p n t", t=PACK),
+                banks[4 + t][:].rearrange("p (t n) -> p n t", t=PACK), gi_b, ALU.mult)
+            nc.vector.tensor_tensor(prod[:, t, :], sig[t][:], win_c[t][:, 0:H], ALU.mult)
+        z2_q = tl([P, N], U32, "z2_q")
+        z2_s = tl([P, N], U8, "z2_s")
+        nc.vector.quantize_mx(out=z2_q[:].bitcast(FP8X4), scales=z2_s[:], in_=z2_bf[:])
+
+        z_bf = [tl([P, P * PACK], BF16, "z_bf%d" % u) for u in range(4)]
+        z_q = [tl([P, P], U32, "z_q%d" % u) for u in range(4)]
+        z_s = [tl([P, P], U8, "z_s%d" % u) for u in range(4)]
+        prod_v = prod[:].rearrange("p t (q u e) -> p u q t e", u=4, e=2)
+        other_v = other[:].rearrange("p t (q u e) -> p u q t e", u=4, e=2)
+        for u in range(4):
+            nc.vector.tensor_tensor(z_bf[u][:].rearrange("p (q e t) -> p q t e", e=2, t=PACK), prod_v[:, u], other_v[:, u], ALU.max)
+            if u > 0:
+                nc.vector.quantize_mx(out=z_q[u - 1][:].bitcast(FP8X4), scales=z_s[u - 1][:], in_=z_bf[u - 1][:])
+        nc.vector.quantize_mx(out=z_q[3][:].bitcast(FP8X4), scales=z_s[3][:], in_=z_bf[3][:])
+
+        cv_half = [tl([P, N], F32, "cv_half%d" % u) for u in range(4)]
+        st_neg = [tl([P, N], F32, "st_neg%d" % u) for u in range(4)]
+        res = [tl([P, N], F32, "res%d" % u) for u in range(4)]
+        out_v = out.rearrange("(q u e) n -> u e q n", u=4, e=2)
+        for u in range(4):
+            nc.tensor.matmul_mx(out=banks[u][:], lhsT=z_q[u][:].bitcast(FP8X4), lhsT_scale=z_s[u][:],
+                                rhs=z2_q[:].bitcast(FP8X4), rhs_scale=z2_s[:], start=True, stop=True)
+            nc.scalar.activation(win_a[u][:, 0:N], banks[u][:], ACT.Copy, scale=0.03125)
+            nc.scalar.activation(cv_half[u][:], banks[u][:], ACT.Copy, scale=0.03125)
+        for u in range(5):
+            if u < 4:
+                nc.vector.tensor_tensor(win_c[u][:, 0:N], win_a[u][:].indirect(lists["n3"][:]), cv_half[u][:], ALU.subtract)
+                nc.scalar.activation(st_neg[u][:], win_c[u][:, 0:N], ACT.Copy, scale=2.0)
+            if u > 0:
+                w = u - 1
+                nc.vector.tensor_tensor(res[w][:], win_c[w][:].indirect(lists["n3"][:]), st_neg[w][:], ALU.subtract)
+                for e in range(2):
+                    nc.sync.dma_start(out_v[w, e], res[w][e:P:2, :])

@@ -1,6 +1,7 @@
 from contextlib import ExitStack
 
 import concourse.mybir as mybir
+from concourse.masks import make_identity
 
 K, T, S, N, H = 512, 2048, 512, 512, 512
 FLOPS = 2 * K * S * H + 2 * K * S * N + 2 * S * H * N
@@ -34,79 +35,105 @@ def tile_picked_momgmaxtwice_none_p_kernel(tc, x_words, x_scales, wa, wb, gt, gi
             lists[name] = keep.tile([P, S // 16], U16, name="list_" + name)
         xs = tl([P, T], U8, "xs")
         xw = tl([P, T], U32, "xw")
-        nc.vector.memset(xs[:].bitcast(I32), 0)
+        nc.gpsimd.memset(xs[:].bitcast(I32), 0)
 
         half = H // 2
-        wa_raw = [tl([P, PACK, half], F32, "wa_raw%d" % h) for h in range(2)]
-        wb_raw = [tl([P, PACK, half], F32, "wb_raw%d" % h) for h in range(2)]
-        gt_sb = tl([P, PACK], F32, "gt_sb")
-        gi_sb = tl([P, PACK], F32, "gi_sb")
+        gt_rows = tl([P, P], F32, "gt_rows")
+        gi_rows = tl([P, P], F32, "gi_rows")
+        nc.gpsimd.memset(gt_rows[:], 0.0)
+        nc.gpsimd.memset(gi_rows[:], 0.0)
+        ident = tl([P, P], F32, "ident")
+        make_identity(nc, ident[:])
+        banks = [psum.tile([P, 512], F32, name="bank%d" % b) for b in range(8)]
 
-        nc.sync.dma_start(lists["offs"][:], offs)
-        for q in range(4):
-            nc.scalar.dma_start(xs[32 * q : 32 * q + 4, :].bitcast(I32), x_scales[0, 4 * q : 4 * q + 4, :].bitcast(I32))
+        for name, src in (("offs", offs), ("two", two), ("n1", n1), ("n2", n2), ("n3", n3)):
+            nc.sync.dma_start(lists[name][:], src)
         nc.sync.dma_start(xw[:].bitcast(I32), x_words[0].rearrange("p n t -> p (n t)").bitcast(I32))
-        nc.sync.dma_start(lists["two"][:], two)
         wa_v = wa.rearrange("(p j) c -> p j c", j=PACK)
         wb_v = wb.rearrange("(p j) c -> p j c", j=PACK)
+        wa_raw = [tl([P, PACK, half], F32, "wa_raw%d" % h)[:] for h in range(2)]
         for h in range(2):
-            nc.sync.dma_start(wa_raw[h][:], wa_v[:, :, h * half : (h + 1) * half])
-        nc.sync.dma_start(gt_sb[:], gt.rearrange("(p t) o -> p (t o)", t=PACK))
-        nc.sync.dma_start(gi_sb[:], gi.rearrange("(p t) o -> p (t o)", t=PACK))
-        nc.sync.dma_start(lists["n1"][:], n1)
-        nc.sync.dma_start(lists["n2"][:], n2)
-        for h in range(2):
-            nc.sync.dma_start(wb_raw[h][:], wb_v[:, :, h * half : (h + 1) * half])
-        nc.sync.dma_start(lists["n3"][:], n3)
+            nc.sync.dma_start(wa_raw[h], wa_v[:, :, h * half : (h + 1) * half])
+        for q in range(4):
+            nc.scalar.dma_start(xs[32 * q : 32 * q + 4, :].bitcast(I32), x_scales[0, 4 * q : 4 * q + 4, :].bitcast(I32))
+
+        def load_rows(queue, rows, g):
+            queue.dma_start(rows[0:PACK, :].rearrange("t (a l) -> t a l", l=4), g.rearrange("(a t l) o -> t a (l o)", t=PACK, l=4))
+
+        load_rows(nc.scalar, gt_rows, gt)
+        wb_raw = [tl([P, PACK, half], F32, "wb_raw%d" % h)[:] for h in range(2)]
+        nc.sync.dma_start(wb_raw[0], wb_v[:, :, 0:half])
+        load_rows(nc.sync, gi_rows, gi)
+        nc.sync.dma_start(wb_raw[1], wb_v[:, :, half:N])
 
         win_a = [tl([P, WIN], F32, "win_a%d" % t) for t in range(PACK)]
         win_c = [tl([P, WIN], F32, "win_c%d" % t) for t in range(PACK)]
-        for t in range(PACK):
-            nc.vector.memset(win_a[t][:, H:WIN], 0.0)
-            nc.vector.memset(win_c[t][:, H:WIN], 0.0)
-
+        zeros = tl([P, WIN - H], F32, "zeros")
+        nc.vector.memset(zeros[:], 0.0)
+        for w in win_a + win_c:
+            nc.vector.tensor_copy(w[:, H:WIN], zeros[:])
         warm = tl([P, 1], F32, "warm")
         nc.scalar.activation(warm[:], win_a[0][:, H : H + 1], ACT.Sigmoid)
 
-        sgn2 = tl([P, PACK], F32, "sgn2")
-        sgn = tl([P, PACK], F32, "sgn")
         gt_abs = tl([P, PACK], F32, "gt_abs")
-        gi_sgn = tl([P, PACK], F32, "gi_sgn")
-        nc.gpsimd.tensor_scalar(sgn2[:], gt_sb[:], 0.0, 2.0, ALU.is_ge, ALU.mult)
-        nc.gpsimd.tensor_scalar(sgn[:], sgn2[:], 1.0, -1.0, ALU.mult, ALU.add)
-        nc.gpsimd.tensor_tensor(gt_abs[:], gt_sb[:], sgn[:], ALU.mult)
-        nc.gpsimd.tensor_tensor(gi_sgn[:], gi_sb[:], sgn[:], ALU.mult)
+        nc.tensor.transpose(banks[0][:, 0:P], gt_rows[:], ident[:])
+        nc.scalar.activation(gt_abs[:], banks[0][:, 0:PACK], ACT.Abs)
+        gt_sign = tl([P, PACK], F32, "gt_sign")
+        nc.scalar.activation(gt_sign[:], banks[0][:, 0:PACK], ACT.Sign)
 
         words = {}
         scales = {}
-        for name in ("offs", "two"):
-            picked = tl([P, S], U8, "picked_" + name)
+
+        def pick_words(name):
+            words[name] = tl([P, S], U32, "words_" + name)
+            nc.vector.tensor_copy(words[name][:].rearrange("p (t a l) -> p a t l", t=PACK, l=4), xw[:].indirect(lists[name][:]))
+
+        def pick_scales(name, tag):
+            picked = keep.tile([P, S], U8, name="picked_" + name, tag=tag, align_bytes=64)
             scales[name] = tl([P, S], U8, "scales_" + name)
             nc.vector.tensor_copy(picked[:], xs[:].indirect(lists[name][:]))
-            nc.vector.tensor_copy(scales[name][:].rearrange("p (t m) -> p t m", t=PACK), picked[:].rearrange("p (m t) -> p t m", t=PACK))
-        for name in ("offs", "two"):
-            words[name] = tl([P, S], U32, "words_" + name)
-            nc.vector.tensor_copy(words[name][:].rearrange("p (t m) -> p m t", t=PACK), xw[:].indirect(lists[name][:]))
+            nc.vector.tensor_copy(scales[name][:].bitcast(I32).rearrange("p (t a) -> p t a", t=PACK), picked[:].bitcast(I32).rearrange("p (a t) -> p t a", t=PACK))
+
+        pick_words("offs")
+        pick_words("two")
+        pick_scales("offs", "picked_offs")
 
         def interleave(copy, dst, raw, h):
             copy(
                 dst[:, h * half * PACK : (h + 1) * half * PACK].rearrange("p (c i t) -> p c t i", i=4, t=PACK),
-                raw[:].rearrange("p t (c i) -> p c t i", i=4),
+                raw.rearrange("p t (c i) -> p c t i", i=4),
             )
 
-        wa_bf = tl([P, H * PACK], BF16, "wa_bf")
+        wa_bf = keep.tile([P, H * PACK], BF16, name="wa_bf", tag="slot_c", align_bytes=64)
         wa_q = tl([P, H], U32, "wa_q")
         wa_s = tl([P, H], U8, "wa_s")
         for h in range(2):
             interleave(nc.scalar.copy, wa_bf, wa_raw[h], h)
         nc.vector.quantize_mx(out=wa_q[:].bitcast(FP8X4), scales=wa_s[:], in_=wa_bf[:])
 
-        banks = [psum.tile([P, 512], F32, name="bank%d" % b) for b in range(8)]
         for t in range(PACK):
             cols = slice(t * P, (t + 1) * P)
             nc.tensor.matmul_mx(out=banks[t][:], lhsT=words["offs"][:, cols].bitcast(FP8X4), lhsT_scale=scales["offs"][:, cols],
                                 rhs=wa_q[:].bitcast(FP8X4), rhs_scale=wa_s[:], start=True, stop=True)
 
+        sig = [tl([P, H], F32, "sig%d" % t) for t in range(PACK)]
+        prod = tl([P, PACK, H], F32, "prod")
+        other = tl([P, PACK, H], F32, "other")
+        def look(t):
+            nc.scalar.activation(sig[t][:], win_a[t][:].indirect(lists["n1"][:]), ACT.Sigmoid)
+            nc.gpsimd.tensor_tensor(prod[:, t, :], sig[t][:], win_c[t][:, 0:H], ALU.mult)
+
+        for t in range(PACK):
+            nc.scalar.copy(win_a[t][:, 0:H], banks[t][:])
+            nc.gpsimd.tensor_scalar(win_c[t][:, 0:H], win_a[t][:, 0:H], gt_abs[:, t : t + 1], 0.0, ALU.mult, ALU.add)
+            nc.vector.tensor_copy(other[:, t, :], win_c[t][:].indirect(lists["n2"][:]))
+            if t > 0:
+                look(t - 1)
+        look(PACK - 1)
+        gi_sgn = tl([P, PACK], F32, "gi_sgn")
+        nc.tensor.transpose(banks[4][:, 0:P], gi_rows[:], ident[:])
+        nc.vector.tensor_tensor(gi_sgn[:], banks[4][:, 0:PACK], gt_sign[:], ALU.mult)
+        pick_scales("two", "slot_c")
         wb_bf = tl([P, N * PACK], BF16, "wb_bf")
         wb_q = tl([P, N], U32, "wb_q")
         wb_s = tl([P, N], U8, "wb_s")
@@ -120,20 +147,12 @@ def tile_picked_momgmaxtwice_none_p_kernel(tc, x_words, x_scales, wa, wb, gt, gi
                 nc.tensor.matmul_mx(out=banks[4 + c][:, cols], lhsT=words["two"][:, cols].bitcast(FP8X4), lhsT_scale=scales["two"][:, cols],
                                     rhs=wb_q[:, ncols].bitcast(FP8X4), rhs_scale=wb_s[:, ncols], start=True, stop=True)
 
-        sig = [tl([P, H], F32, "sig%d" % t) for t in range(PACK)]
-        prod = tl([P, PACK, H], F32, "prod")
-        other = tl([P, PACK, H], F32, "other")
         z2_bf = tl([P, N * PACK], BF16, "z2_bf")
         gi_b = gi_sgn[:].rearrange("p (a t) -> p a t", a=1).to_broadcast([P, P, PACK])
-        for t in range(PACK):
-            nc.scalar.activation(win_c[t][:, 0:H], banks[t][:], ACT.Copy, scale=gt_abs[:, t : t + 1])
-            nc.scalar.copy(win_a[t][:, 0:H], banks[t][:])
-            nc.scalar.activation(sig[t][:], win_a[t][:].indirect(lists["n1"][:]), ACT.Sigmoid)
-            nc.vector.tensor_copy(other[:, t, :], win_c[t][:].indirect(lists["n2"][:]))
+        for c in range(4):
             nc.vector.tensor_tensor(
-                z2_bf[:, t * P * PACK : (t + 1) * P * PACK].rearrange("p (n t) -> p n t", t=PACK),
-                banks[4 + t][:].rearrange("p (t n) -> p n t", t=PACK), gi_b, ALU.mult)
-            nc.vector.tensor_tensor(prod[:, t, :], sig[t][:], win_c[t][:, 0:H], ALU.mult)
+                z2_bf[:, c * P * PACK : (c + 1) * P * PACK].rearrange("p (n t) -> p n t", t=PACK),
+                banks[4 + c][:].rearrange("p (t n) -> p n t", t=PACK), gi_b, ALU.mult)
         z2_q = tl([P, N], U32, "z2_q")
         z2_s = tl([P, N], U8, "z2_s")
         nc.vector.quantize_mx(out=z2_q[:].bitcast(FP8X4), scales=z2_s[:], in_=z2_bf[:])
@@ -164,6 +183,11 @@ def tile_picked_momgmaxtwice_none_p_kernel(tc, x_words, x_scales, wa, wb, gt, gi
                 nc.scalar.activation(st_neg[u][:], win_c[u][:, 0:N], ACT.Copy, scale=2.0)
             if u > 0:
                 w = u - 1
-                nc.vector.tensor_tensor(res[w][:], win_c[w][:].indirect(lists["n3"][:]), st_neg[w][:], ALU.subtract)
-                for e in range(2):
-                    nc.sync.dma_start(out_v[w, e], res[w][e:P:2, :])
+                pieces = 2 if w == 3 else 1
+                width = N // pieces
+                for c in range(pieces):
+                    cols = slice(c * width, (c + 1) * width)
+                    nc.vector.tensor_tensor(res[w][:, cols], win_c[w][:].indirect(lists["n3"][:, c * width // 16 : (c + 1) * width // 16]), st_neg[w][:, cols], ALU.subtract)
+                    for e in range(2):
+                        queue = nc.scalar if (w == 3 and e == 1) else nc.sync
+                        queue.dma_start(out_v[w, e][:, cols], res[w][e:P:2, cols])

@@ -33,6 +33,9 @@ def tile_picked_momgmaxtwice_none_p_kernel(tc, x_words, x_scales, wa, wb, gt, gi
         lists = {}
         for name in ("offs", "two", "n1", "n2", "n3"):
             lists[name] = keep.tile([P, S // 16], U16, name="list_" + name)
+        seed = keep.tile([P, 1], F32, name="seed", tag="slot_a", align_bytes=64)
+        nc.gpsimd.memset(seed[:], 0.0)
+        xs_raw = tl([P, T], U8, "xs_raw")
         xs = tl([P, T], U8, "xs")
         xw = tl([P, T], U32, "xw")
         nc.gpsimd.memset(xs[:].bitcast(I32), 0)
@@ -46,57 +49,59 @@ def tile_picked_momgmaxtwice_none_p_kernel(tc, x_words, x_scales, wa, wb, gt, gi
         make_identity(nc, ident[:])
         banks = [psum.tile([P, 512], F32, name="bank%d" % b) for b in range(8)]
 
-        for name, src in (("offs", offs), ("two", two), ("n1", n1), ("n2", n2), ("n3", n3)):
-            nc.sync.dma_start(lists[name][:], src)
-        nc.sync.dma_start(xw[:].bitcast(I32), x_words[0].rearrange("p n t -> p (n t)").bitcast(I32))
+        for q in range(4):
+            nc.sync.dma_start(xs_raw[32 * q : 32 * q + 4, :].bitcast(I32), x_scales[0, 4 * q : 4 * q + 4, :].bitcast(I32))
+        nc.sync.dma_start(lists["offs"][:], offs)
+        nc.sync.dma_start(lists["two"][:], two)
         wa_v = wa.rearrange("(p j) c -> p j c", j=PACK)
         wb_v = wb.rearrange("(p j) c -> p j c", j=PACK)
         wa_raw = [tl([P, PACK, half], F32, "wa_raw%d" % h)[:] for h in range(2)]
         for h in range(2):
             nc.sync.dma_start(wa_raw[h], wa_v[:, :, h * half : (h + 1) * half])
-        for q in range(4):
-            nc.scalar.dma_start(xs[32 * q : 32 * q + 4, :].bitcast(I32), x_scales[0, 4 * q : 4 * q + 4, :].bitcast(I32))
+        nc.sync.dma_start(xw[:].bitcast(I32), x_words[0].rearrange("p n t -> p (n t)").bitcast(I32))
+        for name, src in (("n1", n1), ("n2", n2), ("n3", n3)):
+            nc.sync.dma_start(lists[name][:], src)
+        for rows, g in ((gt_rows, gt), (gi_rows, gi)):
+            nc.sync.dma_start(rows[0:PACK, :].rearrange("t (a l) -> t a l", l=4), g.rearrange("(a t l) o -> t a (l o)", t=PACK, l=4))
 
-        def load_rows(queue, rows, g):
-            queue.dma_start(rows[0:PACK, :].rearrange("t (a l) -> t a l", l=4), g.rearrange("(a t l) o -> t a (l o)", t=PACK, l=4))
-
-        load_rows(nc.scalar, gt_rows, gt)
-        wb_raw = [tl([P, PACK, half], F32, "wb_raw%d" % h)[:] for h in range(2)]
-        nc.sync.dma_start(wb_raw[0], wb_v[:, :, 0:half])
-        load_rows(nc.sync, gi_rows, gi)
-        nc.sync.dma_start(wb_raw[1], wb_v[:, :, half:N])
-
+        warm = tl([P, 1], F32, "warm")
+        nc.scalar.activation(warm[:], seed[:], ACT.Sigmoid)
         win_a = [tl([P, WIN], F32, "win_a%d" % t) for t in range(PACK)]
         win_c = [tl([P, WIN], F32, "win_c%d" % t) for t in range(PACK)]
-        zeros = tl([P, WIN - H], F32, "zeros")
+        zeros = keep.tile([P, WIN - H], F32, name="zeros", tag="slot_b", align_bytes=64)
         nc.vector.memset(zeros[:], 0.0)
-        for w in win_a + win_c:
-            nc.vector.tensor_copy(w[:, H:WIN], zeros[:])
-        warm = tl([P, 1], F32, "warm")
-        nc.scalar.activation(warm[:], win_a[0][:, H : H + 1], ACT.Sigmoid)
+        for t in range(PACK):
+            nc.vector.tensor_copy(win_a[t][:, H:WIN], zeros[:])
+            nc.scalar.copy(win_c[t][:, H:WIN], zeros[:])
+        wb_raw = [keep.tile([P, PACK, half], F32, name="wb_raw%d" % h, tag=("slot_a", "slot_b")[h], align_bytes=64)[:] for h in range(2)]
+        for h in range(2):
+            nc.sync.dma_start(wb_raw[h], wb_v[:, :, h * half : (h + 1) * half])
+
+        for q in range(4):
+            rows = slice(32 * q, 32 * q + 4)
+            nc.vector.tensor_copy(xs[rows, :].bitcast(I32), xs_raw[rows, :].bitcast(I32))
 
         gt_abs = tl([P, PACK], F32, "gt_abs")
-        nc.tensor.transpose(banks[0][:, 0:P], gt_rows[:], ident[:])
-        nc.scalar.activation(gt_abs[:], banks[0][:, 0:PACK], ACT.Abs)
+        nc.tensor.transpose(banks[3][:, 0:P], gt_rows[:], ident[:])
+        nc.scalar.activation(gt_abs[:], banks[3][:, 0:PACK], ACT.Abs)
         gt_sign = tl([P, PACK], F32, "gt_sign")
-        nc.scalar.activation(gt_sign[:], banks[0][:, 0:PACK], ACT.Sign)
+        nc.scalar.activation(gt_sign[:], banks[3][:, 0:PACK], ACT.Sign)
 
         words = {}
         scales = {}
+        picked = {}
 
         def pick_words(name):
             words[name] = tl([P, S], U32, "words_" + name)
             nc.vector.tensor_copy(words[name][:].rearrange("p (t a l) -> p a t l", t=PACK, l=4), xw[:].indirect(lists[name][:]))
 
-        def pick_scales(name, tag):
-            picked = keep.tile([P, S], U8, name="picked_" + name, tag=tag, align_bytes=64)
+        for name in ("offs", "two"):
+            picked[name] = tl([P, S], U8, "picked_" + name)
+            nc.vector.tensor_copy(picked[name][:], xs[:].indirect(lists[name][:]))
+        for name in ("offs", "two"):
             scales[name] = tl([P, S], U8, "scales_" + name)
-            nc.vector.tensor_copy(picked[:], xs[:].indirect(lists[name][:]))
-            nc.vector.tensor_copy(scales[name][:].bitcast(I32).rearrange("p (t a) -> p t a", t=PACK), picked[:].bitcast(I32).rearrange("p (a t) -> p t a", t=PACK))
-
+            nc.vector.tensor_copy(scales[name][:].bitcast(I32).rearrange("p (t a) -> p t a", t=PACK), picked[name][:].bitcast(I32).rearrange("p (a t) -> p t a", t=PACK))
         pick_words("offs")
-        pick_words("two")
-        pick_scales("offs", "picked_offs")
 
         def interleave(copy, dst, raw, h):
             copy(
@@ -104,7 +109,7 @@ def tile_picked_momgmaxtwice_none_p_kernel(tc, x_words, x_scales, wa, wb, gt, gi
                 raw.rearrange("p t (c i) -> p c t i", i=4),
             )
 
-        wa_bf = keep.tile([P, H * PACK], BF16, name="wa_bf", tag="slot_c", align_bytes=64)
+        wa_bf = tl([P, H * PACK], BF16, "wa_bf")
         wa_q = tl([P, H], U32, "wa_q")
         wa_s = tl([P, H], U8, "wa_s")
         for h in range(2):
@@ -121,43 +126,49 @@ def tile_picked_momgmaxtwice_none_p_kernel(tc, x_words, x_scales, wa, wb, gt, gi
         other = tl([P, PACK, H], F32, "other")
         def look(t):
             nc.scalar.activation(sig[t][:], win_a[t][:].indirect(lists["n1"][:]), ACT.Sigmoid)
-            nc.gpsimd.tensor_tensor(prod[:, t, :], sig[t][:], win_c[t][:, 0:H], ALU.mult)
+            nc.vector.tensor_tensor(prod[:, t, :], sig[t][:], win_c[t][:, 0:H], ALU.mult)
 
         for t in range(PACK):
+            nc.scalar.activation(win_c[t][:, 0:H], banks[t][:], ACT.Copy, scale=gt_abs[:, t : t + 1])
             nc.scalar.copy(win_a[t][:, 0:H], banks[t][:])
-            nc.gpsimd.tensor_scalar(win_c[t][:, 0:H], win_a[t][:, 0:H], gt_abs[:, t : t + 1], 0.0, ALU.mult, ALU.add)
             nc.vector.tensor_copy(other[:, t, :], win_c[t][:].indirect(lists["n2"][:]))
-            if t > 0:
-                look(t - 1)
-        look(PACK - 1)
+            look(t)
         gi_sgn = tl([P, PACK], F32, "gi_sgn")
         nc.tensor.transpose(banks[4][:, 0:P], gi_rows[:], ident[:])
         nc.vector.tensor_tensor(gi_sgn[:], banks[4][:, 0:PACK], gt_sign[:], ALU.mult)
-        pick_scales("two", "slot_c")
+        pick_words("two")
         wb_bf = tl([P, N * PACK], BF16, "wb_bf")
         wb_q = tl([P, N], U32, "wb_q")
         wb_s = tl([P, N], U8, "wb_s")
-        interleave(nc.scalar.copy, wb_bf, wb_raw[0], 0)
+        interleave(nc.vector.tensor_copy, wb_bf, wb_raw[0], 0)
         interleave(nc.vector.tensor_copy, wb_bf, wb_raw[1], 1)
         nc.vector.quantize_mx(out=wb_q[:].bitcast(FP8X4), scales=wb_s[:], in_=wb_bf[:])
-        for c in range(4):
+        for c in range(2):
             ncols = slice(c * P, (c + 1) * P)
             for t in range(PACK):
                 cols = slice(t * P, (t + 1) * P)
                 nc.tensor.matmul_mx(out=banks[4 + c][:, cols], lhsT=words["two"][:, cols].bitcast(FP8X4), lhsT_scale=scales["two"][:, cols],
                                     rhs=wb_q[:, ncols].bitcast(FP8X4), rhs_scale=wb_s[:, ncols], start=True, stop=True)
+        for t in range(PACK):
+            cols = slice(t * P, (t + 1) * P)
+            nc.tensor.matmul_mx(out=banks[6 + t // 2][:, (t % 2) * half : (t % 2 + 1) * half], lhsT=words["two"][:, cols].bitcast(FP8X4), lhsT_scale=scales["two"][:, cols],
+                                rhs=wb_q[:, half:N].bitcast(FP8X4), rhs_scale=wb_s[:, half:N], start=True, stop=True)
 
-        z2_bf = tl([P, N * PACK], BF16, "z2_bf")
+        z2_bf = keep.tile([P, N * PACK], BF16, name="z2_bf", tag="slot_d", align_bytes=64)
         gi_b = gi_sgn[:].rearrange("p (a t) -> p a t", a=1).to_broadcast([P, P, PACK])
-        for c in range(4):
+        for c in range(2):
             nc.vector.tensor_tensor(
                 z2_bf[:, c * P * PACK : (c + 1) * P * PACK].rearrange("p (n t) -> p n t", t=PACK),
                 banks[4 + c][:].rearrange("p (t n) -> p n t", t=PACK), gi_b, ALU.mult)
+        z2_rows = tl([P, PACK, half], BF16, "z2_rows")
+        for t in range(PACK):
+            nc.scalar.activation(z2_rows[:, t, :], banks[6 + t // 2][:, (t % 2) * half : (t % 2 + 1) * half], ACT.Copy, scale=gi_sgn[:, t : t + 1])
+        interleave(nc.scalar.copy, z2_bf, z2_rows[:], 1)
         z2_q = tl([P, N], U32, "z2_q")
         z2_s = tl([P, N], U8, "z2_s")
         nc.vector.quantize_mx(out=z2_q[:].bitcast(FP8X4), scales=z2_s[:], in_=z2_bf[:])
 
-        z_bf = [tl([P, P * PACK], BF16, "z_bf%d" % u) for u in range(4)]
+        z_bf = [keep.tile([P, P * PACK], BF16, name="z_bf%d" % u, tag="slot_d" if u == 2 else "z_bf%d" % u, align_bytes=64) for u in range(4)]
         z_q = [tl([P, P], U32, "z_q%d" % u) for u in range(4)]
         z_s = [tl([P, P], U8, "z_s%d" % u) for u in range(4)]
         prod_v = prod[:].rearrange("p t (q u e) -> p u q t e", u=4, e=2)

@@ -33,18 +33,17 @@ def tile_picked_momgmaxtwice_none_p_kernel(tc, x_words, x_scales, wa, wb, gt, gi
         lists = {}
         for name in ("offs", "two", "n1", "n2", "n3"):
             lists[name] = keep.tile([P, S // 16], U16, name="list_" + name)
+        half = H // 2
+        gt_rows = tl([P, P], F32, "gt_rows")
+        nc.gpsimd.memset(gt_rows[:], 0.0)
         seed = keep.tile([P, 1], F32, name="seed", tag="slot_a", align_bytes=64)
         nc.gpsimd.memset(seed[:], 0.0)
+        gi_rows = tl([P, P], F32, "gi_rows")
+        nc.gpsimd.memset(gi_rows[:], 0.0)
         xs_raw = tl([P, T], U8, "xs_raw")
         xs = tl([P, T], U8, "xs")
         xw = tl([P, T], U32, "xw")
         nc.gpsimd.memset(xs[:].bitcast(I32), 0)
-
-        half = H // 2
-        gt_rows = tl([P, P], F32, "gt_rows")
-        gi_rows = tl([P, P], F32, "gi_rows")
-        nc.gpsimd.memset(gt_rows[:], 0.0)
-        nc.gpsimd.memset(gi_rows[:], 0.0)
         ident = tl([P, P], F32, "ident")
         make_identity(nc, ident[:])
         banks = [psum.tile([P, 512], F32, name="bank%d" % b) for b in range(8)]
@@ -52,17 +51,21 @@ def tile_picked_momgmaxtwice_none_p_kernel(tc, x_words, x_scales, wa, wb, gt, gi
         for q in range(4):
             nc.sync.dma_start(xs_raw[32 * q : 32 * q + 4, :].bitcast(I32), x_scales[0, 4 * q : 4 * q + 4, :].bitcast(I32))
         nc.sync.dma_start(lists["offs"][:], offs)
-        nc.sync.dma_start(lists["two"][:], two)
         wa_v = wa.rearrange("(p j) c -> p j c", j=PACK)
         wb_v = wb.rearrange("(p j) c -> p j c", j=PACK)
         wa_raw = [tl([P, PACK, half], F32, "wa_raw%d" % h)[:] for h in range(2)]
         for h in range(2):
             nc.sync.dma_start(wa_raw[h], wa_v[:, :, h * half : (h + 1) * half])
+
+        def load_rows(rows, g):
+            nc.sync.dma_start(rows[0:PACK, :].rearrange("t (a l) -> t a l", l=4), g.rearrange("(a t l) o -> t a (l o)", t=PACK, l=4))
+
+        load_rows(gt_rows, gt)
+        nc.sync.dma_start(lists["two"][:], two)
         nc.sync.dma_start(xw[:].bitcast(I32), x_words[0].rearrange("p n t -> p (n t)").bitcast(I32))
+        load_rows(gi_rows, gi)
         for name, src in (("n1", n1), ("n2", n2), ("n3", n3)):
             nc.sync.dma_start(lists[name][:], src)
-        for rows, g in ((gt_rows, gt), (gi_rows, gi)):
-            nc.sync.dma_start(rows[0:PACK, :].rearrange("t (a l) -> t a l", l=4), g.rearrange("(a t l) o -> t a (l o)", t=PACK, l=4))
 
         warm = tl([P, 1], F32, "warm")
         nc.scalar.activation(warm[:], seed[:], ACT.Sigmoid)
@@ -82,10 +85,14 @@ def tile_picked_momgmaxtwice_none_p_kernel(tc, x_words, x_scales, wa, wb, gt, gi
             nc.vector.tensor_copy(xs[rows, :].bitcast(I32), xs_raw[rows, :].bitcast(I32))
 
         gt_abs = tl([P, PACK], F32, "gt_abs")
-        nc.tensor.transpose(banks[3][:, 0:P], gt_rows[:], ident[:])
-        nc.scalar.activation(gt_abs[:], banks[3][:, 0:PACK], ACT.Abs)
+        nc.tensor.transpose(banks[0][:, 0:P], gt_rows[:], ident[:])
+        nc.scalar.activation(gt_abs[:], banks[0][:, 0:PACK], ACT.Abs)
         gt_sign = tl([P, PACK], F32, "gt_sign")
-        nc.scalar.activation(gt_sign[:], banks[3][:, 0:PACK], ACT.Sign)
+        nc.scalar.activation(gt_sign[:], banks[0][:, 0:PACK], ACT.Sign)
+
+        gt_wide = [tl([P, H], F32, "gt_wide%d" % t) for t in range(PACK)]
+        for t in range(PACK):
+            nc.scalar.activation(gt_wide[t][:], win_c[t][:, H:WIN], ACT.Identity, bias=gt_abs[:, t : t + 1])
 
         words = {}
         scales = {}
@@ -121,26 +128,22 @@ def tile_picked_momgmaxtwice_none_p_kernel(tc, x_words, x_scales, wa, wb, gt, gi
             nc.tensor.matmul_mx(out=banks[t][:], lhsT=words["offs"][:, cols].bitcast(FP8X4), lhsT_scale=scales["offs"][:, cols],
                                 rhs=wa_q[:].bitcast(FP8X4), rhs_scale=wa_s[:], start=True, stop=True)
 
+        wb_bf = tl([P, N * PACK], BF16, "wb_bf")
+        interleave(nc.scalar.copy, wb_bf, wb_raw[0], 0)
         sig = [tl([P, H], F32, "sig%d" % t) for t in range(PACK)]
         prod = tl([P, PACK, H], F32, "prod")
         other = tl([P, PACK, H], F32, "other")
-        def look(t):
-            nc.scalar.activation(sig[t][:], win_a[t][:].indirect(lists["n1"][:]), ACT.Sigmoid)
-            nc.vector.tensor_tensor(prod[:, t, :], sig[t][:], win_c[t][:, 0:H], ALU.mult)
-
         for t in range(PACK):
-            nc.scalar.activation(win_c[t][:, 0:H], banks[t][:], ACT.Copy, scale=gt_abs[:, t : t + 1])
             nc.scalar.copy(win_a[t][:, 0:H], banks[t][:])
-            nc.vector.tensor_copy(other[:, t, :], win_c[t][:].indirect(lists["n2"][:]))
-            look(t)
+            nc.vector.tensor_tensor(other[:, t, :], win_a[t][:].indirect(lists["n2"][:]), gt_wide[t][:], ALU.mult)
+            nc.scalar.activation(sig[t][:], win_a[t][:].indirect(lists["n1"][:]), ACT.Sigmoid)
+            nc.vector.scalar_tensor_tensor(prod[:, t, :], sig[t][:], gt_abs[:, t : t + 1], win_a[t][:, 0:H], ALU.mult, ALU.mult)
         gi_sgn = tl([P, PACK], F32, "gi_sgn")
         nc.tensor.transpose(banks[4][:, 0:P], gi_rows[:], ident[:])
         nc.vector.tensor_tensor(gi_sgn[:], banks[4][:, 0:PACK], gt_sign[:], ALU.mult)
         pick_words("two")
-        wb_bf = tl([P, N * PACK], BF16, "wb_bf")
         wb_q = tl([P, N], U32, "wb_q")
         wb_s = tl([P, N], U8, "wb_s")
-        interleave(nc.vector.tensor_copy, wb_bf, wb_raw[0], 0)
         interleave(nc.vector.tensor_copy, wb_bf, wb_raw[1], 1)
         nc.vector.quantize_mx(out=wb_q[:].bitcast(FP8X4), scales=wb_s[:], in_=wb_bf[:])
         for c in range(2):

@@ -18,7 +18,14 @@ ACT = mybir.ActivationFunctionType
 
 P = 128
 PACK = 4
+QUADS = 4
+RUN = 4
+PAIR = 2
+BANK = 512
+HALF = 256
 WIN = 1024
+SCALAR_FILLS = 2
+HELD_ROW_TILE = 2
 
 
 def tile_picked_momgmaxtwice_none_p_kernel(tc, x_words, x_scales, wa, wb, gt, gi, offs, two, n1, n2, n3, out):
@@ -27,181 +34,188 @@ def tile_picked_momgmaxtwice_none_p_kernel(tc, x_words, x_scales, wa, wb, gt, gi
         keep = ctx.enter_context(tc.tile_pool(name="keep", bufs=1))
         psum = ctx.enter_context(tc.psum_pool(name="psum", bufs=1))
 
-        def tl(shape, dt, name):
-            return keep.tile(shape, dt, name=name, align_bytes=64)
+        def tile(shape, dtype, name, tag=None):
+            return keep.tile(shape, dtype, name=name, tag=tag or name, align_bytes=64)
 
-        lists = {}
-        for name in ("offs", "two", "n1", "n2", "n3"):
-            lists[name] = keep.tile([P, S // 16], U16, name="list_" + name)
-        half = H // 2
-        gt_rows = tl([P, P], F32, "gt_rows")
-        nc.gpsimd.memset(gt_rows[:], 0.0)
-        seed = keep.tile([P, 1], F32, name="seed", tag="slot_a", align_bytes=64)
-        nc.gpsimd.memset(seed[:], 0.0)
-        gi_rows = tl([P, P], F32, "gi_rows")
-        nc.gpsimd.memset(gi_rows[:], 0.0)
-        xs_raw = tl([P, T], U8, "xs_raw")
-        xs = tl([P, T], U8, "xs")
-        xw = tl([P, T], U32, "xw")
-        nc.gpsimd.memset(xs[:].bitcast(I32), 0)
-        ident = tl([P, P], F32, "ident")
-        make_identity(nc, ident[:])
-        banks = [psum.tile([P, 512], F32, name="bank%d" % b) for b in range(8)]
+        def product(dst, lhs, lhs_scales, rhs, rhs_scales):
+            nc.tensor.matmul_mx(out=dst, lhsT=lhs.bitcast(FP8X4), lhsT_scale=lhs_scales,
+                                rhs=rhs.bitcast(FP8X4), rhs_scale=rhs_scales, start=True, stop=True)
 
-        for q in range(4):
-            nc.sync.dma_start(xs_raw[32 * q : 32 * q + 4, :].bitcast(I32), x_scales[0, 4 * q : 4 * q + 4, :].bitcast(I32))
-        nc.sync.dma_start(lists["offs"][:], offs)
-        wa_v = wa.rearrange("(p j) c -> p j c", j=PACK)
-        wb_v = wb.rearrange("(p j) c -> p j c", j=PACK)
-        wa_raw = [tl([P, PACK, half], F32, "wa_raw%d" % h)[:] for h in range(2)]
-        for h in range(2):
-            nc.sync.dma_start(wa_raw[h], wa_v[:, :, h * half : (h + 1) * half])
+        def quantize(codes, scale_bytes, values):
+            nc.vector.quantize_mx(out=codes[:].bitcast(FP8X4), scales=scale_bytes[:], in_=values[:])
 
-        def load_rows(rows, g):
-            nc.sync.dma_start(rows[0:PACK, :].rearrange("t (a l) -> t a l", l=4), g.rearrange("(a t l) o -> t a (l o)", t=PACK, l=4))
-
-        load_rows(gt_rows, gt)
-        nc.sync.dma_start(lists["two"][:], two)
-        nc.sync.dma_start(xw[:].bitcast(I32), x_words[0].rearrange("p n t -> p (n t)").bitcast(I32))
-        load_rows(gi_rows, gi)
-        for name, src in (("n1", n1), ("n2", n2), ("n3", n3)):
-            nc.sync.dma_start(lists[name][:], src)
-
-        warm = tl([P, 1], F32, "warm")
-        nc.scalar.activation(warm[:], seed[:], ACT.Sigmoid)
-        win_a = [tl([P, WIN], F32, "win_a%d" % t) for t in range(PACK)]
-        win_c = [tl([P, WIN], F32, "win_c%d" % t) for t in range(PACK)]
-        zeros = keep.tile([P, WIN - H], F32, name="zeros", tag="slot_b", align_bytes=64)
-        nc.vector.memset(zeros[:], 0.0)
-        for t in range(PACK):
-            nc.vector.tensor_copy(win_a[t][:, H:WIN], zeros[:])
-            nc.scalar.copy(win_c[t][:, H:WIN], zeros[:])
-        wb_raw = [keep.tile([P, PACK, half], F32, name="wb_raw%d" % h, tag=("slot_a", "slot_b")[h], align_bytes=64)[:] for h in range(2)]
-        for h in range(2):
-            nc.sync.dma_start(wb_raw[h], wb_v[:, :, h * half : (h + 1) * half])
-
-        for q in range(4):
-            rows = slice(32 * q, 32 * q + 4)
-            nc.vector.tensor_copy(xs[rows, :].bitcast(I32), xs_raw[rows, :].bitcast(I32))
-
-        gt_abs = tl([P, PACK], F32, "gt_abs")
-        nc.tensor.transpose(banks[0][:, 0:P], gt_rows[:], ident[:])
-        nc.scalar.activation(gt_abs[:], banks[0][:, 0:PACK], ACT.Abs)
-        gt_sign = tl([P, PACK], F32, "gt_sign")
-        nc.scalar.activation(gt_sign[:], banks[0][:, 0:PACK], ACT.Sign)
-
-        gt_wide = [tl([P, H], F32, "gt_wide%d" % t) for t in range(PACK)]
-        for t in range(PACK):
-            nc.scalar.activation(gt_wide[t][:], win_c[t][:, H:WIN], ACT.Identity, bias=gt_abs[:, t : t + 1])
-
-        words = {}
-        scales = {}
-        picked = {}
-
-        def pick_words(name):
-            words[name] = tl([P, S], U32, "words_" + name)
-            nc.vector.tensor_copy(words[name][:].rearrange("p (t a l) -> p a t l", t=PACK, l=4), xw[:].indirect(lists[name][:]))
-
-        for name in ("offs", "two"):
-            picked[name] = tl([P, S], U8, "picked_" + name)
-            nc.vector.tensor_copy(picked[name][:], xs[:].indirect(lists[name][:]))
-        for name in ("offs", "two"):
-            scales[name] = tl([P, S], U8, "scales_" + name)
-            nc.vector.tensor_copy(scales[name][:].bitcast(I32).rearrange("p (t a) -> p t a", t=PACK), picked[name][:].bitcast(I32).rearrange("p (a t) -> p t a", t=PACK))
-        pick_words("offs")
-
-        def interleave(copy, dst, raw, h):
+        def interleave(copy, dst, rows, h):
             copy(
-                dst[:, h * half * PACK : (h + 1) * half * PACK].rearrange("p (c i t) -> p c t i", i=4, t=PACK),
-                raw.rearrange("p t (c i) -> p c t i", i=4),
+                dst[:, h * HALF * PACK : (h + 1) * HALF * PACK].rearrange("p (c i j) -> p c j i", i=RUN, j=PACK),
+                rows.rearrange("p j (c i) -> p c j i", i=RUN),
             )
 
-        wa_bf = tl([P, H * PACK], BF16, "wa_bf")
-        wa_q = tl([P, H], U32, "wa_q")
-        wa_s = tl([P, H], U8, "wa_s")
+        lists = {name: keep.tile([P, S // 16], U16, name="list_" + name) for name in ("offs", "two", "n1", "n2", "n3")}
+
+        gt_rows = tile([P, P], F32, "gt_rows", tag="gt_rows_then_wb")
+        nc.gpsimd.memset(gt_rows[:], 0.0)
+        gi_rows = tile([P, P], F32, "gi_rows")
+        nc.gpsimd.memset(gi_rows[:], 0.0)
+        x_bytes_raw = tile([P, T], U8, "x_bytes_raw")
+        x_bytes = tile([P, T], U8, "x_bytes")
+        x_codes = tile([P, T], U32, "x_codes")
+        nc.gpsimd.memset(x_bytes[:].bitcast(I32), 0)
+        ident = tile([P, P], F32, "ident")
+        make_identity(nc, ident[:])
+        banks = [psum.tile([P, BANK], F32, name="bank%d" % b) for b in range(2 * PACK)]
+
+        def load_rows(rows, factor):
+            nc.sync.dma_start(rows[0:PACK, :].rearrange("t (c l) -> t c l", l=RUN),
+                              factor.rearrange("(c t l) o -> t c (l o)", t=PACK, l=RUN))
+
+        for quad in range(QUADS):
+            nc.sync.dma_start(x_bytes_raw[32 * quad : 32 * quad + 4, :].bitcast(I32),
+                              x_scales[0, 4 * quad : 4 * quad + 4, :].bitcast(I32))
+        nc.sync.dma_start(lists["offs"][:], offs)
+        wa_rows = wa.rearrange("(p j) c -> p j c", j=PACK)
+        wb_rows = wb.rearrange("(p j) c -> p j c", j=PACK)
+        wa_raw = [tile([P, PACK, HALF], F32, "wa_raw%d" % h) for h in range(2)]
         for h in range(2):
-            interleave(nc.scalar.copy, wa_bf, wa_raw[h], h)
-        nc.vector.quantize_mx(out=wa_q[:].bitcast(FP8X4), scales=wa_s[:], in_=wa_bf[:])
+            nc.sync.dma_start(wa_raw[h][:], wa_rows[:, :, h * HALF : (h + 1) * HALF])
+        load_rows(gt_rows, gt)
+        nc.sync.dma_start(lists["two"][:], two)
+        nc.sync.dma_start(x_codes[:].bitcast(I32), x_words[0].rearrange("p n j -> p (n j)").bitcast(I32))
+        load_rows(gi_rows, gi)
+        for name, source in (("n1", n1), ("n2", n2), ("n3", n3)):
+            nc.sync.dma_start(lists[name][:], source)
 
-        for t in range(PACK):
-            cols = slice(t * P, (t + 1) * P)
-            nc.tensor.matmul_mx(out=banks[t][:], lhsT=words["offs"][:, cols].bitcast(FP8X4), lhsT_scale=scales["offs"][:, cols],
-                                rhs=wa_q[:].bitcast(FP8X4), rhs_scale=wa_s[:], start=True, stop=True)
+        first_win = [tile([P, WIN], F32, "first_win%d" % t) for t in range(PACK)]
+        second_win = [tile([P, WIN], F32, "second_win%d" % t) for t in range(PACK)]
+        zeros = tile([P, WIN - H], F32, "zeros", tag="zeros_then_wb")
+        nc.vector.memset(zeros[:], 0.0)
+        windows = first_win + second_win
+        for window in windows[:SCALAR_FILLS]:
+            nc.scalar.activation(window[:, H:WIN], zeros[:], ACT.Sigmoid)
+        for window in windows[SCALAR_FILLS:]:
+            nc.vector.tensor_copy(window[:, H:WIN], zeros[:])
 
-        wb_bf = tl([P, N * PACK], BF16, "wb_bf")
-        interleave(nc.scalar.copy, wb_bf, wb_raw[0], 0)
-        sig = [tl([P, H], F32, "sig%d" % t) for t in range(PACK)]
-        prod = tl([P, PACK, H], F32, "prod")
-        other = tl([P, PACK, H], F32, "other")
+        for quad in range(QUADS):
+            rows = slice(32 * quad, 32 * quad + 4)
+            nc.vector.tensor_copy(x_bytes[rows, :].bitcast(I32), x_bytes_raw[rows, :].bitcast(I32))
+
+        gt_abs = tile([P, PACK], F32, "gt_abs")
+        gt_sign = tile([P, PACK], F32, "gt_sign")
+        nc.tensor.transpose(banks[0][:, 0:P], gt_rows[:], ident[:])
+        nc.scalar.activation(gt_abs[:], banks[0][:, 0:PACK], ACT.Abs)
+        nc.scalar.activation(gt_sign[:], banks[0][:, 0:PACK], ACT.Sign)
+
+        wb_raw = [tile([P, PACK, HALF], F32, "wb_raw%d" % h, tag=tag)
+                  for h, tag in enumerate(("zeros_then_wb", "gt_rows_then_wb"))]
+        for h in range(2):
+            nc.sync.dma_start(wb_raw[h][:], wb_rows[:, :, h * HALF : (h + 1) * HALF])
+
+        codes = {name: tile([P, S], U32, "codes_" + name) for name in ("offs", "two")}
+        picked = {name: tile([P, S], U8, "picked_" + name) for name in ("offs", "two")}
+        scales = {name: tile([P, S], U8, "scales_" + name) for name in ("offs", "two")}
+
+        def pick_codes(name):
+            nc.vector.tensor_copy(codes[name][:].rearrange("p (t c l) -> p c t l", t=PACK, l=RUN),
+                                  x_codes[:].indirect(lists[name][:]))
+
+        for name in ("offs", "two"):
+            nc.vector.tensor_copy(picked[name][:], x_bytes[:].indirect(lists[name][:]))
+        for name in ("offs", "two"):
+            nc.vector.tensor_copy(scales[name][:].bitcast(I32).rearrange("p (t c) -> p t c", t=PACK),
+                                  picked[name][:].bitcast(I32).rearrange("p (c t) -> p t c", t=PACK))
+        pick_codes("offs")
+
+        wa_bf = tile([P, H * PACK], BF16, "wa_bf")
+        wa_codes = tile([P, H], U32, "wa_codes")
+        wa_scales = tile([P, H], U8, "wa_scales")
+        for h in range(2):
+            interleave(nc.scalar.copy, wa_bf, wa_raw[h][:], h)
+        quantize(wa_codes, wa_scales, wa_bf)
+        places = [slice(t * P, (t + 1) * P) for t in range(PACK)]
         for t in range(PACK):
-            nc.scalar.copy(win_a[t][:, 0:H], banks[t][:])
-            nc.vector.tensor_tensor(other[:, t, :], win_a[t][:].indirect(lists["n2"][:]), gt_wide[t][:], ALU.mult)
-            nc.scalar.activation(sig[t][:], win_a[t][:].indirect(lists["n1"][:]), ACT.Sigmoid)
-            nc.vector.scalar_tensor_tensor(prod[:, t, :], sig[t][:], gt_abs[:, t : t + 1], win_a[t][:, 0:H], ALU.mult, ALU.mult)
-        gi_sgn = tl([P, PACK], F32, "gi_sgn")
-        nc.tensor.transpose(banks[4][:, 0:P], gi_rows[:], ident[:])
-        nc.vector.tensor_tensor(gi_sgn[:], banks[4][:, 0:PACK], gt_sign[:], ALU.mult)
-        pick_words("two")
-        wb_q = tl([P, N], U32, "wb_q")
-        wb_s = tl([P, N], U8, "wb_s")
-        interleave(nc.vector.tensor_copy, wb_bf, wb_raw[1], 1)
-        nc.vector.quantize_mx(out=wb_q[:].bitcast(FP8X4), scales=wb_s[:], in_=wb_bf[:])
-        for c in range(2):
-            ncols = slice(c * P, (c + 1) * P)
+            product(banks[t][:], codes["offs"][:, places[t]], scales["offs"][:, places[t]], wa_codes[:], wa_scales[:])
+
+        gate = [tile([P, H], F32, "gate%d" % t) for t in range(PACK)]
+        gated = tile([P, PACK, H], F32, "gated")
+        other = tile([P, PACK, H], F32, "other")
+        for t in range(PACK):
+            nc.scalar.activation(second_win[t][:, 0:H], banks[t][:], ACT.Copy, scale=gt_abs[:, t : t + 1])
+            nc.scalar.copy(first_win[t][:, 0:H], banks[t][:])
+            nc.vector.tensor_copy(other[:, t, :], second_win[t][:].indirect(lists["n2"][:]))
+            nc.scalar.activation(gate[t][:], first_win[t][:].indirect(lists["n1"][:]), ACT.Sigmoid)
+            nc.vector.tensor_tensor(gated[:, t, :], gate[t][:], second_win[t][:, 0:H], ALU.mult)
+
+        gi_signed = tile([P, PACK], F32, "gi_signed")
+        nc.tensor.transpose(banks[PACK][:, 0:P], gi_rows[:], ident[:])
+        nc.vector.tensor_tensor(gi_signed[:], banks[PACK][:, 0:PACK], gt_sign[:], ALU.mult)
+        pick_codes("two")
+        wb_bf = tile([P, N * PACK], BF16, "wb_bf")
+        wb_codes = tile([P, N], U32, "wb_codes")
+        wb_scales = tile([P, N], U8, "wb_scales")
+        for h in range(2):
+            interleave(nc.vector.tensor_copy, wb_bf, wb_raw[h][:], h)
+        quantize(wb_codes, wb_scales, wb_bf)
+        vector_banks = banks[PACK : PACK + HALF // P]
+        scalar_parts = [banks[PACK + HALF // P + t // 2][:, (t % 2) * HALF : (t % 2 + 1) * HALF] for t in range(PACK)]
+        for part, bank in enumerate(vector_banks):
+            columns = slice(part * P, (part + 1) * P)
             for t in range(PACK):
-                cols = slice(t * P, (t + 1) * P)
-                nc.tensor.matmul_mx(out=banks[4 + c][:, cols], lhsT=words["two"][:, cols].bitcast(FP8X4), lhsT_scale=scales["two"][:, cols],
-                                    rhs=wb_q[:, ncols].bitcast(FP8X4), rhs_scale=wb_s[:, ncols], start=True, stop=True)
+                product(bank[:, places[t]], codes["two"][:, places[t]], scales["two"][:, places[t]],
+                        wb_codes[:, columns], wb_scales[:, columns])
         for t in range(PACK):
-            cols = slice(t * P, (t + 1) * P)
-            nc.tensor.matmul_mx(out=banks[6 + t // 2][:, (t % 2) * half : (t % 2 + 1) * half], lhsT=words["two"][:, cols].bitcast(FP8X4), lhsT_scale=scales["two"][:, cols],
-                                rhs=wb_q[:, half:N].bitcast(FP8X4), rhs_scale=wb_s[:, half:N], start=True, stop=True)
+            product(scalar_parts[t], codes["two"][:, places[t]], scales["two"][:, places[t]],
+                    wb_codes[:, HALF:N], wb_scales[:, HALF:N])
 
-        z2_bf = keep.tile([P, N * PACK], BF16, name="z2_bf", tag="slot_d", align_bytes=64)
-        gi_b = gi_sgn[:].rearrange("p (a t) -> p a t", a=1).to_broadcast([P, P, PACK])
-        for c in range(2):
+        z2_bf = tile([P, N * PACK], BF16, "z2_bf", tag="z2_then_z")
+        gi_along_columns = gi_signed[:].rearrange("p (o t) -> p o t", o=1).to_broadcast([P, P, PACK])
+        for part, bank in enumerate(vector_banks):
             nc.vector.tensor_tensor(
-                z2_bf[:, c * P * PACK : (c + 1) * P * PACK].rearrange("p (n t) -> p n t", t=PACK),
-                banks[4 + c][:].rearrange("p (t n) -> p n t", t=PACK), gi_b, ALU.mult)
-        z2_rows = tl([P, PACK, half], BF16, "z2_rows")
+                z2_bf[:, part * P * PACK : (part + 1) * P * PACK].rearrange("p (n t) -> p n t", t=PACK),
+                bank[:].rearrange("p (t n) -> p n t", t=PACK), gi_along_columns, ALU.mult)
+        z2_rows = tile([P, PACK, HALF], BF16, "z2_rows")
         for t in range(PACK):
-            nc.scalar.activation(z2_rows[:, t, :], banks[6 + t // 2][:, (t % 2) * half : (t % 2 + 1) * half], ACT.Copy, scale=gi_sgn[:, t : t + 1])
+            nc.scalar.activation(z2_rows[:, t, :], scalar_parts[t], ACT.Copy, scale=gi_signed[:, t : t + 1])
         interleave(nc.scalar.copy, z2_bf, z2_rows[:], 1)
-        z2_q = tl([P, N], U32, "z2_q")
-        z2_s = tl([P, N], U8, "z2_s")
-        nc.vector.quantize_mx(out=z2_q[:].bitcast(FP8X4), scales=z2_s[:], in_=z2_bf[:])
+        z2_codes = tile([P, N], U32, "z2_codes")
+        z2_scales = tile([P, N], U8, "z2_scales")
+        quantize(z2_codes, z2_scales, z2_bf)
 
-        z_bf = [keep.tile([P, P * PACK], BF16, name="z_bf%d" % u, tag="slot_d" if u == 2 else "z_bf%d" % u, align_bytes=64) for u in range(4)]
-        z_q = [tl([P, P], U32, "z_q%d" % u) for u in range(4)]
-        z_s = [tl([P, P], U8, "z_s%d" % u) for u in range(4)]
-        prod_v = prod[:].rearrange("p t (q u e) -> p u q t e", u=4, e=2)
-        other_v = other[:].rearrange("p t (q u e) -> p u q t e", u=4, e=2)
-        for u in range(4):
-            nc.vector.tensor_tensor(z_bf[u][:].rearrange("p (q e t) -> p q t e", e=2, t=PACK), prod_v[:, u], other_v[:, u], ALU.max)
-            if u > 0:
-                nc.vector.quantize_mx(out=z_q[u - 1][:].bitcast(FP8X4), scales=z_s[u - 1][:], in_=z_bf[u - 1][:])
-        nc.vector.quantize_mx(out=z_q[3][:].bitcast(FP8X4), scales=z_s[3][:], in_=z_bf[3][:])
+        z_bf = [tile([P, P * PACK], BF16, "z_bf%d" % u, tag="z2_then_z" if u == HELD_ROW_TILE else None) for u in range(PACK)]
+        z_codes = [tile([P, P], U32, "z_codes%d" % u) for u in range(PACK)]
+        z_scales = [tile([P, P], U8, "z_scales%d" % u) for u in range(PACK)]
+        gated_dealt = gated[:].rearrange("p t (q u e) -> p u q t e", u=PACK, e=PAIR)
+        other_dealt = other[:].rearrange("p t (q u e) -> p u q t e", u=PACK, e=PAIR)
+        for step in range(PACK + 1):
+            if step < PACK:
+                nc.vector.tensor_tensor(z_bf[step][:].rearrange("p (q e t) -> p q t e", e=PAIR, t=PACK),
+                                        gated_dealt[:, step], other_dealt[:, step], ALU.max)
+            if step > 0:
+                quantize(z_codes[step - 1], z_scales[step - 1], z_bf[step - 1])
 
-        cv_half = [tl([P, N], F32, "cv_half%d" % u) for u in range(4)]
-        st_neg = [tl([P, N], F32, "st_neg%d" % u) for u in range(4)]
-        res = [tl([P, N], F32, "res%d" % u) for u in range(4)]
-        out_v = out.rearrange("(q u e) n -> u e q n", u=4, e=2)
-        for u in range(4):
-            nc.tensor.matmul_mx(out=banks[u][:], lhsT=z_q[u][:].bitcast(FP8X4), lhsT_scale=z_s[u][:],
-                                rhs=z2_q[:].bitcast(FP8X4), rhs_scale=z2_s[:], start=True, stop=True)
-            nc.scalar.activation(win_a[u][:, 0:N], banks[u][:], ACT.Copy, scale=0.03125)
-            nc.scalar.activation(cv_half[u][:], banks[u][:], ACT.Copy, scale=0.03125)
-        for u in range(5):
-            if u < 4:
-                nc.vector.tensor_tensor(win_c[u][:, 0:N], win_a[u][:].indirect(lists["n3"][:]), cv_half[u][:], ALU.subtract)
-                nc.scalar.activation(st_neg[u][:], win_c[u][:, 0:N], ACT.Copy, scale=2.0)
-            if u > 0:
-                w = u - 1
-                pieces = 2 if w == 3 else 1
-                width = N // pieces
-                for c in range(pieces):
-                    cols = slice(c * width, (c + 1) * width)
-                    nc.vector.tensor_tensor(res[w][:, cols], win_c[w][:].indirect(lists["n3"][:, c * width // 16 : (c + 1) * width // 16]), st_neg[w][:, cols], ALU.subtract)
-                    for e in range(2):
-                        queue = nc.scalar if (w == 3 and e == 1) else nc.sync
-                        queue.dma_start(out_v[w, e][:, cols], res[w][e:P:2, cols])
+        cv_half = [tile([P, N], F32, "cv_half%d" % u) for u in range(PACK)]
+        st_neg = [tile([P, N], F32, "st_neg%d" % u) for u in range(PACK)]
+        result = [tile([P, N], F32, "result%d" % u) for u in range(PACK)]
+        out_dealt = out.rearrange("(q u e) n -> u e q n", u=PACK, e=PAIR)
+        for u in range(PACK):
+            product(banks[u][:], z_codes[u][:], z_scales[u][:], z2_codes[:], z2_scales[:])
+            nc.scalar.activation(first_win[u][:, 0:N], banks[u][:], ACT.Copy, scale=0.0625 / 2)
+            nc.scalar.activation(cv_half[u][:], banks[u][:], ACT.Copy, scale=0.0625 / 2)
+
+        def finish(u):
+            last = u == PACK - 1
+            width = N // 2 if last else N
+            for start in range(0, N, width):
+                columns = slice(start, start + width)
+                entries = lists["n3"][:, start // 16 : (start + width) // 16]
+                nc.vector.tensor_tensor(result[u][:, columns], second_win[u][:].indirect(entries),
+                                        st_neg[u][:, columns], ALU.subtract)
+                for e in range(PAIR):
+                    queue = nc.scalar if (last and e == 1) else nc.sync
+                    queue.dma_start(out_dealt[u, e][:, columns], result[u][e:P:PAIR, columns])
+
+        for step in range(PACK + 1):
+            if step < PACK:
+                nc.vector.tensor_tensor(second_win[step][:, 0:N], first_win[step][:].indirect(lists["n3"][:]),
+                                        cv_half[step][:], ALU.subtract)
+                nc.scalar.activation(st_neg[step][:], second_win[step][:, 0:N], ACT.Copy, scale=2.0)
+            if step > 0:
+                finish(step - 1)

from contextlib import ExitStack

import concourse.mybir as mybir
from concourse.masks import make_identity

K, T, S, N, H = 512, 2048, 512, 512, 512
FLOPS = 2 * K * S * H + 2 * K * S * N + 2 * S * H * N

F32 = mybir.dt.float32
BF16 = mybir.dt.bfloat16
I32 = mybir.dt.int32
U32 = mybir.dt.uint32
U16 = mybir.dt.uint16
U8 = mybir.dt.uint8
FP8X4 = mybir.dt.float8_e4m3fn_x4
ALU = mybir.AluOpType
ACT = mybir.ActivationFunctionType

P = 128
PACK = 4
QUADS = 4
RUN = 4
PAIR = 2
BANK = 512
HALF = 256
WIN = 1024
SCALAR_FILLS = 2
HELD_ROW_TILE = 2


def tile_picked_momgmaxtwice_none_p_kernel(tc, x_words, x_scales, wa, wb, gt, gi, offs, two, n1, n2, n3, out):
    nc = tc.nc
    with ExitStack() as ctx:
        keep = ctx.enter_context(tc.tile_pool(name="keep", bufs=1))
        psum = ctx.enter_context(tc.psum_pool(name="psum", bufs=1))

        def tile(shape, dtype, name, tag=None):
            return keep.tile(shape, dtype, name=name, tag=tag or name, align_bytes=64)

        def product(dst, lhs, lhs_scales, rhs, rhs_scales):
            nc.tensor.matmul_mx(out=dst, lhsT=lhs.bitcast(FP8X4), lhsT_scale=lhs_scales,
                                rhs=rhs.bitcast(FP8X4), rhs_scale=rhs_scales, start=True, stop=True)

        def quantize(codes, scale_bytes, values):
            nc.vector.quantize_mx(out=codes[:].bitcast(FP8X4), scales=scale_bytes[:], in_=values[:])

        def interleave(copy, dst, rows, h):
            copy(
                dst[:, h * HALF * PACK : (h + 1) * HALF * PACK].rearrange("p (c i j) -> p c j i", i=RUN, j=PACK),
                rows.rearrange("p j (c i) -> p c j i", i=RUN),
            )

        lists = {name: keep.tile([P, S // 16], U16, name="list_" + name) for name in ("offs", "two", "n1", "n2", "n3")}

        gt_rows = tile([P, P], F32, "gt_rows", tag="gt_rows_then_wb")
        nc.gpsimd.memset(gt_rows[:], 0.0)
        gi_rows = tile([P, P], F32, "gi_rows")
        nc.gpsimd.memset(gi_rows[:], 0.0)
        x_bytes_raw = tile([P, T], U8, "x_bytes_raw")
        x_bytes = tile([P, T], U8, "x_bytes")
        x_codes = tile([P, T], U32, "x_codes")
        nc.gpsimd.memset(x_bytes[:].bitcast(I32), 0)
        ident = tile([P, P], F32, "ident")
        make_identity(nc, ident[:])
        banks = [psum.tile([P, BANK], F32, name="bank%d" % b) for b in range(2 * PACK)]

        def load_rows(rows, factor):
            nc.sync.dma_start(rows[0:PACK, :].rearrange("t (c l) -> t c l", l=RUN),
                              factor.rearrange("(c t l) o -> t c (l o)", t=PACK, l=RUN))

        for quad in range(QUADS):
            nc.sync.dma_start(x_bytes_raw[32 * quad : 32 * quad + 4, :].bitcast(I32),
                              x_scales[0, 4 * quad : 4 * quad + 4, :].bitcast(I32))
        nc.sync.dma_start(lists["offs"][:], offs)
        wa_rows = wa.rearrange("(p j) c -> p j c", j=PACK)
        wb_rows = wb.rearrange("(p j) c -> p j c", j=PACK)
        wa_raw = [tile([P, PACK, HALF], F32, "wa_raw%d" % h) for h in range(2)]
        for h in range(2):
            nc.sync.dma_start(wa_raw[h][:], wa_rows[:, :, h * HALF : (h + 1) * HALF])
        load_rows(gt_rows, gt)
        nc.sync.dma_start(lists["two"][:], two)
        nc.sync.dma_start(x_codes[:].bitcast(I32), x_words[0].rearrange("p n j -> p (n j)").bitcast(I32))
        load_rows(gi_rows, gi)
        for name, source in (("n1", n1), ("n2", n2), ("n3", n3)):
            nc.sync.dma_start(lists[name][:], source)

        first_win = [tile([P, WIN], F32, "first_win%d" % t) for t in range(PACK)]
        second_win = [tile([P, WIN], F32, "second_win%d" % t) for t in range(PACK)]
        zeros = tile([P, WIN - H], F32, "zeros", tag="zeros_then_wb")
        nc.vector.memset(zeros[:], 0.0)
        windows = first_win + second_win
        for window in windows[:SCALAR_FILLS]:
            nc.scalar.activation(window[:, H:WIN], zeros[:], ACT.Sigmoid)
        for window in windows[SCALAR_FILLS:]:
            nc.vector.tensor_copy(window[:, H:WIN], zeros[:])

        for quad in range(QUADS):
            rows = slice(32 * quad, 32 * quad + 4)
            nc.vector.tensor_copy(x_bytes[rows, :].bitcast(I32), x_bytes_raw[rows, :].bitcast(I32))

        gt_abs = tile([P, PACK], F32, "gt_abs")
        gt_sign = tile([P, PACK], F32, "gt_sign")
        nc.tensor.transpose(banks[0][:, 0:P], gt_rows[:], ident[:])
        nc.scalar.activation(gt_abs[:], banks[0][:, 0:PACK], ACT.Abs)
        nc.scalar.activation(gt_sign[:], banks[0][:, 0:PACK], ACT.Sign)

        wb_raw = [tile([P, PACK, HALF], F32, "wb_raw%d" % h, tag=tag)
                  for h, tag in enumerate(("zeros_then_wb", "gt_rows_then_wb"))]
        for h in range(2):
            nc.sync.dma_start(wb_raw[h][:], wb_rows[:, :, h * HALF : (h + 1) * HALF])

        codes = {name: tile([P, S], U32, "codes_" + name) for name in ("offs", "two")}
        picked = {name: tile([P, S], U8, "picked_" + name) for name in ("offs", "two")}
        scales = {name: tile([P, S], U8, "scales_" + name) for name in ("offs", "two")}

        def pick_codes(name):
            nc.vector.tensor_copy(codes[name][:].rearrange("p (t c l) -> p c t l", t=PACK, l=RUN),
                                  x_codes[:].indirect(lists[name][:]))

        for name in ("offs", "two"):
            nc.vector.tensor_copy(picked[name][:], x_bytes[:].indirect(lists[name][:]))
        for name in ("offs", "two"):
            nc.vector.tensor_copy(scales[name][:].bitcast(I32).rearrange("p (t c) -> p t c", t=PACK),
                                  picked[name][:].bitcast(I32).rearrange("p (c t) -> p t c", t=PACK))
        pick_codes("offs")

        wa_bf = tile([P, H * PACK], BF16, "wa_bf")
        wa_codes = tile([P, H], U32, "wa_codes")
        wa_scales = tile([P, H], U8, "wa_scales")
        for h in range(2):
            interleave(nc.scalar.copy, wa_bf, wa_raw[h][:], h)
        quantize(wa_codes, wa_scales, wa_bf)
        places = [slice(t * P, (t + 1) * P) for t in range(PACK)]
        for t in range(PACK):
            product(banks[t][:], codes["offs"][:, places[t]], scales["offs"][:, places[t]], wa_codes[:], wa_scales[:])

        gate = [tile([P, H], F32, "gate%d" % t) for t in range(PACK)]
        gated = tile([P, PACK, H], F32, "gated")
        other = tile([P, PACK, H], F32, "other")
        for t in range(PACK):
            nc.scalar.activation(second_win[t][:, 0:H], banks[t][:], ACT.Copy, scale=gt_abs[:, t : t + 1])
            nc.scalar.copy(first_win[t][:, 0:H], banks[t][:])
            nc.vector.tensor_copy(other[:, t, :], second_win[t][:].indirect(lists["n2"][:]))
            nc.scalar.activation(gate[t][:], first_win[t][:].indirect(lists["n1"][:]), ACT.Sigmoid)
            nc.vector.tensor_tensor(gated[:, t, :], gate[t][:], second_win[t][:, 0:H], ALU.mult)

        gi_signed = tile([P, PACK], F32, "gi_signed")
        nc.tensor.transpose(banks[PACK][:, 0:P], gi_rows[:], ident[:])
        nc.vector.tensor_tensor(gi_signed[:], banks[PACK][:, 0:PACK], gt_sign[:], ALU.mult)
        pick_codes("two")
        wb_bf = tile([P, N * PACK], BF16, "wb_bf")
        wb_codes = tile([P, N], U32, "wb_codes")
        wb_scales = tile([P, N], U8, "wb_scales")
        for h in range(2):
            interleave(nc.vector.tensor_copy, wb_bf, wb_raw[h][:], h)
        quantize(wb_codes, wb_scales, wb_bf)
        vector_banks = banks[PACK : PACK + HALF // P]
        scalar_parts = [banks[PACK + HALF // P + t // 2][:, (t % 2) * HALF : (t % 2 + 1) * HALF] for t in range(PACK)]
        for part, bank in enumerate(vector_banks):
            columns = slice(part * P, (part + 1) * P)
            for t in range(PACK):
                product(bank[:, places[t]], codes["two"][:, places[t]], scales["two"][:, places[t]],
                        wb_codes[:, columns], wb_scales[:, columns])
        for t in range(PACK):
            product(scalar_parts[t], codes["two"][:, places[t]], scales["two"][:, places[t]],
                    wb_codes[:, HALF:N], wb_scales[:, HALF:N])

        z2_bf = tile([P, N * PACK], BF16, "z2_bf", tag="z2_then_z")
        gi_along_columns = gi_signed[:].rearrange("p (o t) -> p o t", o=1).to_broadcast([P, P, PACK])
        for part, bank in enumerate(vector_banks):
            nc.vector.tensor_tensor(
                z2_bf[:, part * P * PACK : (part + 1) * P * PACK].rearrange("p (n t) -> p n t", t=PACK),
                bank[:].rearrange("p (t n) -> p n t", t=PACK), gi_along_columns, ALU.mult)
        z2_rows = tile([P, PACK, HALF], BF16, "z2_rows")
        for t in range(PACK):
            nc.scalar.activation(z2_rows[:, t, :], scalar_parts[t], ACT.Copy, scale=gi_signed[:, t : t + 1])
        interleave(nc.scalar.copy, z2_bf, z2_rows[:], 1)
        z2_codes = tile([P, N], U32, "z2_codes")
        z2_scales = tile([P, N], U8, "z2_scales")
        quantize(z2_codes, z2_scales, z2_bf)

        z_bf = [tile([P, P * PACK], BF16, "z_bf%d" % u, tag="z2_then_z" if u == HELD_ROW_TILE else None) for u in range(PACK)]
        z_codes = [tile([P, P], U32, "z_codes%d" % u) for u in range(PACK)]
        z_scales = [tile([P, P], U8, "z_scales%d" % u) for u in range(PACK)]
        gated_dealt = gated[:].rearrange("p t (q u e) -> p u q t e", u=PACK, e=PAIR)
        other_dealt = other[:].rearrange("p t (q u e) -> p u q t e", u=PACK, e=PAIR)
        for step in range(PACK + 1):
            if step < PACK:
                nc.vector.tensor_tensor(z_bf[step][:].rearrange("p (q e t) -> p q t e", e=PAIR, t=PACK),
                                        gated_dealt[:, step], other_dealt[:, step], ALU.max)
            if step > 0:
                quantize(z_codes[step - 1], z_scales[step - 1], z_bf[step - 1])

        cv_half = [tile([P, N], F32, "cv_half%d" % u) for u in range(PACK)]
        st_neg = [tile([P, N], F32, "st_neg%d" % u) for u in range(PACK)]
        result = [tile([P, N], F32, "result%d" % u) for u in range(PACK)]
        out_dealt = out.rearrange("(q u e) n -> u e q n", u=PACK, e=PAIR)
        for u in range(PACK):
            product(banks[u][:], z_codes[u][:], z_scales[u][:], z2_codes[:], z2_scales[:])
            nc.scalar.activation(first_win[u][:, 0:N], banks[u][:], ACT.Copy, scale=0.0625 / 2)
            nc.scalar.activation(cv_half[u][:], banks[u][:], ACT.Copy, scale=0.0625 / 2)

        def finish(u):
            last = u == PACK - 1
            width = N // 2 if last else N
            for start in range(0, N, width):
                columns = slice(start, start + width)
                entries = lists["n3"][:, start // 16 : (start + width) // 16]
                nc.vector.tensor_tensor(result[u][:, columns], second_win[u][:].indirect(entries),
                                        st_neg[u][:, columns], ALU.subtract)
                for e in range(PAIR):
                    queue = nc.scalar if (last and e == 1) else nc.sync
                    queue.dma_start(out_dealt[u, e][:, columns], result[u][e:P:PAIR, columns])

        for step in range(PACK + 1):
            if step < PACK:
                nc.vector.tensor_tensor(second_win[step][:, 0:N], first_win[step][:].indirect(lists["n3"][:]),
                                        cv_half[step][:], ALU.subtract)
                nc.scalar.activation(st_neg[step][:], second_win[step][:, 0:N], ACT.Copy, scale=2.0)
            if step > 0:
                finish(step - 1)
